import numpy as np, ml_dtypes
CORES = [78,86,94,102,110,118]
N = 6
TK, NT = 512, 3
def setup_inputs(rng):
    x = rng.standard_normal((NT, 128, TK), dtype=np.float32).astype(ml_dtypes.bfloat16)
    return {"x": np.broadcast_to(x, (2, NT, 128, TK)).reshape(N, 128, TK).copy(), "w": rng.standard_normal((N, 128, NT * 128), dtype=np.float32).astype(ml_dtypes.bfloat16)}
def setup_inputs_big(rng):
    d = setup_inputs(rng)
    for k in ("x", "w"): d[k] = (d[k].astype(np.float32) * 1024.0).astype(d[k].dtype)
    return d
def setup_inputs_small(rng):
    d = setup_inputs(rng)
    for k in ("x", "w"): d[k] = (d[k].astype(np.float32) * (1 / 1024.0)).astype(d[k].dtype)
    return d
def setup_inputs_apart(rng):
    d = setup_inputs(rng)
    f = (10.0 ** rng.permutation(np.linspace(-1.5, 1.5, N))).astype(np.float32).reshape(N, 1, 1)
    for k in ("x", "w"): d[k] = (d[k].astype(np.float32) * f).astype(d[k].dtype)
    return d
def tie_inputs(x):
    x = dict(x)
    x["x"] = np.concatenate([x["x"][:NT], x["x"][:NT]])
    return x
def reference(x, w):
    X, W = x.astype(np.float64), w.astype(np.float64)
    y = np.stack([sum(W[r][:, 128 * j:128 * j + 128].T @ X[j if r < NT else j + NT] for j in range(NT)) for r in range(N)])
    return {"y": y.astype(ml_dtypes.bfloat16 if x.dtype != np.float64 else np.float64)}

@@ -1,0 +1,133 @@
+from concourse.bass import DstId, RemoteDMATransfer
+
+NT = 3
+TK = 512
+H = TK // 2
+
+SCRATCH = {
+    "xt0": ("sbuf", [128, TK], "bfloat16"),
+    "xt1": ("sbuf", [128, TK], "bfloat16"),
+    "xt2": ("sbuf", [128, TK], "bfloat16"),
+    "ws": ("sbuf", [128, NT * 128], "bfloat16"),
+    "ys": ("sbuf", [128, TK], "bfloat16"),
+    "psA": ("psum", [128, 512], "float32"),
+    "psB": ("psum", [128, 512], "float32"),
+}
+SEMAPHORES = ["xl", "wl", "arr0", "arr1", "arr2", "sent", "mmA", "mmB", "cpA", "cpB", "stA", "stB"]
+
+
+def _links(topo, src, dst):
+    a, b, d = topo.chip(src), topo.chip(dst), topo.die(src)
+    if a == b:
+        return []
+    if topo.mates(a, b):
+        return [("mate", a, d)]
+    if topo.same_plane(a, b):
+        return [("out", a, d), ("in", b, d)]
+    m = [c for c in range(topo.CHIPS) if topo.mates(a, c)][0]
+    return [("mate", a, d), ("out", m, d), ("in", b, d)]
+
+
+def _plan(topo, cores):
+    n = len(cores)
+    options = []
+    for j in range(NT):
+        need = [r for r in range(n) if r % NT != j]
+        opts = []
+        for p in range(len(need)):
+            for q in range(p + 1, len(need)):
+                first = [need[p], need[q]]
+                opts.append((first, [r for r in need if r not in first]))
+        options.append(opts)
+    best = None
+    for o0 in options[0]:
+        for o1 in options[1]:
+            for o2 in options[2]:
+                load, crossed, ok, serves = {}, 0, True, {}
+                for j, (a, b) in enumerate((o0, o1, o2)):
+                    for h, ds in ((j, a), (j + NT, b)):
+                        serves[h] = ds
+                        for r in ds:
+                            ok = ok and topo.may_write(cores[h], cores[r])
+                            for l in _links(topo, cores[h], cores[r]):
+                                load[l] = load.get(l, 0) + 1
+                                crossed += 1
+                key = (sorted(load.values(), reverse=True), crossed)
+                if ok and (best is None or key < best[0]):
+                    best = (key, serves)
+    return best[1]
+
+
+def _bits(mask):
+    return [e for e in range(mask.bit_length()) if (mask >> e) & 1]
+
+
+def _mask_of(engines):
+    m = 0
+    for e in engines:
+        m |= 1 << e
+    return m
+
+
+def rank_program(g, core, T, topo):
+    rank = T.rank_of(core)
+    if rank is None:
+        return
+    cores = list(T.cores)
+    serves = _plan(topo, cores)
+    own = rank % NT
+    xt = [T.xt0, T.xt1, T.xt2]
+    arr = [T.sem.arr0, T.sem.arr1, T.sem.arr2]
+
+    g.sync.dma_start(xt[own][:], T.x[:]).then_inc(T.sem.xl, 16)
+    g.scalar.dma_start(T.ws[:], T.w[:]).then_inc(T.sem.wl, 16)
+
+    dsts = [cores[r] for r in serves[rank]]
+    common = topo.mask(core, dsts[0]) & topo.mask(core, dsts[1])
+    eng = _bits(common)
+    half = len(eng) // 2
+    parts = [eng[:half], eng[half:2 * half]]
+    transfers = []
+    for d, e in zip(dsts, parts):
+        rid, pid, _ = topo.addr(d)
+        transfers.append(RemoteDMATransfer(dst_ids=[DstId(rid=rid, pnc=pid)], dma_engine_mask=_mask_of(e),
+                                           remote_sem=arr[own], src=xt[own][:], dst=xt[own][:]))
+    g.wait_ge(T.sem.xl, 16)
+    g.remote_dma_fused(transfers, local_sem=T.sem.sent)
+
+    foreign = []
+    for j in range(NT):
+        if j == own:
+            continue
+        for h in (j, j + NT):
+            if rank in serves[h]:
+                ds = [cores[r] for r in serves[h]]
+                cnt = len(_bits(topo.mask(cores[h], ds[0]) & topo.mask(cores[h], ds[1]))) // 2
+                foreign.append((len(_links(topo, cores[h], core)), j, cnt))
+    foreign.sort()
+
+    halves = [(T.psA, 0, T.sem.mmA), (T.psB, H, T.sem.mmB)]
+    g.tensor.wait_ge(T.sem.xl, 16)
+    g.tensor.wait_ge(T.sem.wl, 16)
+    for ps, c0, _ in halves:
+        g.tensor.matmul(ps[:, 0:H], T.ws[:, 128 * own:128 * own + 128], xt[own][:, c0:c0 + H], True, False)
+    for k, (_, j, cnt) in enumerate(foreign):
+        last = k == len(foreign) - 1
+        g.tensor.wait_ge(arr[j], cnt)
+        for ps, c0, sem in halves:
+            mm = g.tensor.matmul(ps[:, 0:H], T.ws[:, 128 * j:128 * j + 128], xt[j][:, c0:c0 + H], False, last)
+            if last:
+                mm.then_inc(sem, 1)
+
+    g.vector.wait_ge(T.sem.mmA, 1)
+    g.vector.tensor_copy(T.ys[:, 0:H], T.psA[:, 0:H]).then_inc(T.sem.cpA, 1)
+    g.vector.wait_ge(T.sem.mmB, 1)
+    g.vector.tensor_copy(T.ys[:, H:TK], T.psB[:, 0:H]).then_inc(T.sem.cpB, 1)
+
+    g.sync.wait_ge(T.sem.cpA, 1)
+    g.sync.dma_start(T.y[:, 0:H], T.ys[:, 0:H]).then_inc(T.sem.stA, 16)
+    g.scalar.wait_ge(T.sem.cpB, 1)
+    g.scalar.dma_start(T.y[:, H:TK], T.ys[:, H:TK]).then_inc(T.sem.stB, 16)
+    g.sync.wait_ge(T.sem.stA, 16)
+    g.scalar.wait_ge(T.sem.stB, 16)
+    g.wait_ge(T.sem.sent, 2 * half)

@@ -1,8 +1,7 @@
-from concourse.bass import DstId, RemoteDMATransfer
-
 NT = 3
 TK = 512
 H = TK // 2
+Q3 = H + H // 2
 
 SCRATCH = {
     "xt0": ("sbuf", [128, TK], "bfloat16"),
@@ -10,63 +9,23 @@ SCRATCH = {
     "xt2": ("sbuf", [128, TK], "bfloat16"),
     "ws": ("sbuf", [128, NT * 128], "bfloat16"),
     "ys": ("sbuf", [128, TK], "bfloat16"),
-    "psA": ("psum", [128, 512], "float32"),
-    "psB": ("psum", [128, 512], "float32"),
+    "ps0": ("psum", [128, 512], "float32"),
+    "ps1": ("psum", [128, 512], "float32"),
+    "ps2": ("psum", [128, 512], "float32"),
 }
-SEMAPHORES = ["xl", "wl", "arr0", "arr1", "arr2", "sent", "mmA", "mmB", "cpA", "cpB", "stA", "stB"]
+SEMAPHORES = ["xlA", "xlB", "wl", "arr1", "arr2A", "arr2B", "sent",
+              "mm0", "mm1", "mm2", "cp0", "cp1", "cp2", "st0", "st1", "st2"]
 
 
-def _links(topo, src, dst):
-    a, b, d = topo.chip(src), topo.chip(dst), topo.die(src)
-    if a == b:
-        return []
-    if topo.mates(a, b):
-        return [("mate", a, d)]
-    if topo.same_plane(a, b):
-        return [("out", a, d), ("in", b, d)]
-    m = [c for c in range(topo.CHIPS) if topo.mates(a, c)][0]
-    return [("mate", a, d), ("out", m, d), ("in", b, d)]
+def _ring(topo, cores, rank):
+    here = topo.chip(cores[rank])
+    ring = [r for r in range(len(cores)) if r == rank or topo.same_plane(here, topo.chip(cores[r]))]
+    assert sorted(r % NT for r in ring) == list(range(NT))
+    return ring
 
 
-def _plan(topo, cores):
-    n = len(cores)
-    options = []
-    for j in range(NT):
-        need = [r for r in range(n) if r % NT != j]
-        opts = []
-        for p in range(len(need)):
-            for q in range(p + 1, len(need)):
-                first = [need[p], need[q]]
-                opts.append((first, [r for r in need if r not in first]))
-        options.append(opts)
-    best = None
-    for o0 in options[0]:
-        for o1 in options[1]:
-            for o2 in options[2]:
-                load, crossed, ok, serves = {}, 0, True, {}
-                for j, (a, b) in enumerate((o0, o1, o2)):
-                    for h, ds in ((j, a), (j + NT, b)):
-                        serves[h] = ds
-                        for r in ds:
-                            ok = ok and topo.may_write(cores[h], cores[r])
-                            for l in _links(topo, cores[h], cores[r]):
-                                load[l] = load.get(l, 0) + 1
-                                crossed += 1
-                key = (sorted(load.values(), reverse=True), crossed)
-                if ok and (best is None or key < best[0]):
-                    best = (key, serves)
-    return best[1]
-
-
-def _bits(mask):
-    return [e for e in range(mask.bit_length()) if (mask >> e) & 1]
-
-
-def _mask_of(engines):
-    m = 0
-    for e in engines:
-        m |= 1 << e
-    return m
+def _engines(mask):
+    return sum((mask >> e) & 1 for e in range(mask.bit_length()))
 
 
 def rank_program(g, core, T, topo):
@@ -74,60 +33,64 @@ def rank_program(g, core, T, topo):
     if rank is None:
         return
     cores = list(T.cores)
-    serves = _plan(topo, cores)
+    ring = _ring(topo, cores, rank)
+    i = ring.index(rank)
     own = rank % NT
     xt = [T.xt0, T.xt1, T.xt2]
-    arr = [T.sem.arr0, T.sem.arr1, T.sem.arr2]
+    mine = xt[own]
+    S = T.sem
 
-    g.sync.dma_start(xt[own][:], T.x[:]).then_inc(T.sem.xl, 16)
-    g.scalar.dma_start(T.ws[:], T.w[:]).then_inc(T.sem.wl, 16)
+    g.sync.dma_start(mine[:, 0:H], T.x[:, 0:H]).then_inc(S.xlA, 16)
+    g.sync.dma_start(mine[:, H:TK], T.x[:, H:TK]).then_inc(S.xlB, 16)
+    g.sync.dma_start(T.ws[:], T.w[:]).then_inc(S.wl, 16)
 
-    dsts = [cores[r] for r in serves[rank]]
-    common = topo.mask(core, dsts[0]) & topo.mask(core, dsts[1])
-    eng = _bits(common)
-    half = len(eng) // 2
-    parts = [eng[:half], eng[half:2 * half]]
-    transfers = []
-    for d, e in zip(dsts, parts):
+    d1, d2 = cores[ring[(i + 1) % NT]], cores[ring[(i + 2) % NT]]
+    sent = 0
+    for d, c0, c1, sem, loaded in ((d2, 0, H, S.arr2A, S.xlA), (d1, 0, TK, S.arr1, S.xlB), (d2, H, TK, S.arr2B, None)):
+        if loaded is not None:
+            g.wait_ge(loaded, 16)
         rid, pid, _ = topo.addr(d)
-        transfers.append(RemoteDMATransfer(dst_ids=[DstId(rid=rid, pnc=pid)], dma_engine_mask=_mask_of(e),
-                                           remote_sem=arr[own], src=xt[own][:], dst=xt[own][:]))
-    g.wait_ge(T.sem.xl, 16)
-    g.remote_dma_fused(transfers, local_sem=T.sem.sent)
+        m = topo.mask(core, d)
+        g.remote_dma(mine[:, c0:c1], mine[:, c0:c1], sem, S.sent, pid, rid, m)
+        sent += _engines(m)
 
-    foreign = []
-    for j in range(NT):
-        if j == own:
-            continue
-        for h in (j, j + NT):
-            if rank in serves[h]:
-                ds = [cores[r] for r in serves[h]]
-                cnt = len(_bits(topo.mask(cores[h], ds[0]) & topo.mask(cores[h], ds[1]))) // 2
-                foreign.append((len(_links(topo, cores[h], core)), j, cnt))
-    foreign.sort()
+    s1, s2 = ring[(i - 1) % NT], ring[(i - 2) % NT]
+    n1, n2 = _engines(topo.mask(cores[s1], core)), _engines(topo.mask(cores[s2], core))
+    j1, j2 = s1 % NT, s2 % NT
 
-    halves = [(T.psA, 0, T.sem.mmA), (T.psB, H, T.sem.mmB)]
-    g.tensor.wait_ge(T.sem.xl, 16)
-    g.tensor.wait_ge(T.sem.wl, 16)
-    for ps, c0, _ in halves:
-        g.tensor.matmul(ps[:, 0:H], T.ws[:, 128 * own:128 * own + 128], xt[own][:, c0:c0 + H], True, False)
-    for k, (_, j, cnt) in enumerate(foreign):
-        last = k == len(foreign) - 1
-        g.tensor.wait_ge(arr[j], cnt)
-        for ps, c0, sem in halves:
-            mm = g.tensor.matmul(ps[:, 0:H], T.ws[:, 128 * j:128 * j + 128], xt[j][:, c0:c0 + H], False, last)
-            if last:
-                mm.then_inc(sem, 1)
+    groups = [(T.ps0, 0, H, S.mm0, S.cp0, S.st0), (T.ps1, H, Q3, S.mm1, S.cp1, S.st1),
+              (T.ps2, Q3, TK, S.mm2, S.cp2, S.st2)]
 
-    g.vector.wait_ge(T.sem.mmA, 1)
-    g.vector.tensor_copy(T.ys[:, 0:H], T.psA[:, 0:H]).then_inc(T.sem.cpA, 1)
-    g.vector.wait_ge(T.sem.mmB, 1)
-    g.vector.tensor_copy(T.ys[:, H:TK], T.psB[:, 0:H]).then_inc(T.sem.cpB, 1)
+    def mm(k, j, start, stop):
+        ps, c0, c1, done = groups[k][0:4]
+        ins = g.tensor.matmul(ps[:, 0:c1 - c0], T.ws[:, 128 * j:128 * j + 128], xt[j][:, c0:c1], start, stop)
+        if stop:
+            ins.then_inc(done, 1)
 
-    g.sync.wait_ge(T.sem.cpA, 1)
-    g.sync.dma_start(T.y[:, 0:H], T.ys[:, 0:H]).then_inc(T.sem.stA, 16)
-    g.scalar.wait_ge(T.sem.cpB, 1)
-    g.scalar.dma_start(T.y[:, H:TK], T.ys[:, H:TK]).then_inc(T.sem.stB, 16)
-    g.sync.wait_ge(T.sem.stA, 16)
-    g.scalar.wait_ge(T.sem.stB, 16)
-    g.wait_ge(T.sem.sent, 2 * half)
+    g.tensor.wait_ge(S.xlA, 16)
+    g.tensor.wait_ge(S.xlB, 16)
+    g.tensor.wait_ge(S.wl, 16)
+    for k in range(3):
+        mm(k, own, True, False)
+    g.tensor.wait_ge(S.arr2A, n2)
+    mm(0, j2, False, False)
+    g.tensor.wait_ge(S.arr1, n1)
+    mm(0, j1, False, True)
+    mm(1, j1, False, False)
+    mm(2, j1, False, False)
+    g.tensor.wait_ge(S.arr2B, n2)
+    mm(1, j2, False, True)
+    mm(2, j2, False, True)
+
+    for ps, c0, c1, done, copied, _ in groups:
+        g.vector.wait_ge(done, 1)
+        g.vector.tensor_copy(T.ys[:, c0:c1], ps[:, 0:c1 - c0]).then_inc(copied, 1)
+
+    for q, ks in ((g.sync, (0, 1)), (g.scalar, (2,))):
+        for k in ks:
+            _, c0, c1, _, copied, stored = groups[k]
+            q.wait_ge(copied, 1)
+            q.dma_start(T.y[:, c0:c1], T.ys[:, c0:c1]).then_inc(stored, 16)
+        for k in ks:
+            q.wait_ge(groups[k][5], 16)
+    g.wait_ge(S.sent, sent)

NT = 3
TK = 512
H = TK // 2
Q3 = H + H // 2

SCRATCH = {
    "xt0": ("sbuf", [128, TK], "bfloat16"),
    "xt1": ("sbuf", [128, TK], "bfloat16"),
    "xt2": ("sbuf", [128, TK], "bfloat16"),
    "ws": ("sbuf", [128, NT * 128], "bfloat16"),
    "ys": ("sbuf", [128, TK], "bfloat16"),
    "ps0": ("psum", [128, 512], "float32"),
    "ps1": ("psum", [128, 512], "float32"),
    "ps2": ("psum", [128, 512], "float32"),
}
SEMAPHORES = ["xlA", "xlB", "wl", "arr1", "arr2A", "arr2B", "sent",
              "mm0", "mm1", "mm2", "cp0", "cp1", "cp2", "st0", "st1", "st2"]


def _ring(topo, cores, rank):
    here = topo.chip(cores[rank])
    ring = [r for r in range(len(cores)) if r == rank or topo.same_plane(here, topo.chip(cores[r]))]
    assert sorted(r % NT for r in ring) == list(range(NT))
    return ring


def _engines(mask):
    return sum((mask >> e) & 1 for e in range(mask.bit_length()))


def rank_program(g, core, T, topo):
    rank = T.rank_of(core)
    if rank is None:
        return
    cores = list(T.cores)
    ring = _ring(topo, cores, rank)
    i = ring.index(rank)
    own = rank % NT
    xt = [T.xt0, T.xt1, T.xt2]
    mine = xt[own]
    S = T.sem

    g.sync.dma_start(mine[:, 0:H], T.x[:, 0:H]).then_inc(S.xlA, 16)
    g.sync.dma_start(mine[:, H:TK], T.x[:, H:TK]).then_inc(S.xlB, 16)
    g.sync.dma_start(T.ws[:], T.w[:]).then_inc(S.wl, 16)

    d1, d2 = cores[ring[(i + 1) % NT]], cores[ring[(i + 2) % NT]]
    sent = 0
    for d, c0, c1, sem, loaded in ((d2, 0, H, S.arr2A, S.xlA), (d1, 0, TK, S.arr1, S.xlB), (d2, H, TK, S.arr2B, None)):
        if loaded is not None:
            g.wait_ge(loaded, 16)
        rid, pid, _ = topo.addr(d)
        m = topo.mask(core, d)
        g.remote_dma(mine[:, c0:c1], mine[:, c0:c1], sem, S.sent, pid, rid, m)
        sent += _engines(m)

    s1, s2 = ring[(i - 1) % NT], ring[(i - 2) % NT]
    n1, n2 = _engines(topo.mask(cores[s1], core)), _engines(topo.mask(cores[s2], core))
    j1, j2 = s1 % NT, s2 % NT

    groups = [(T.ps0, 0, H, S.mm0, S.cp0, S.st0), (T.ps1, H, Q3, S.mm1, S.cp1, S.st1),
              (T.ps2, Q3, TK, S.mm2, S.cp2, S.st2)]

    def mm(k, j, start, stop):
        ps, c0, c1, done = groups[k][0:4]
        ins = g.tensor.matmul(ps[:, 0:c1 - c0], T.ws[:, 128 * j:128 * j + 128], xt[j][:, c0:c1], start, stop)
        if stop:
            ins.then_inc(done, 1)

    g.tensor.wait_ge(S.xlA, 16)
    g.tensor.wait_ge(S.xlB, 16)
    g.tensor.wait_ge(S.wl, 16)
    for k in range(3):
        mm(k, own, True, False)
    g.tensor.wait_ge(S.arr2A, n2)
    mm(0, j2, False, False)
    g.tensor.wait_ge(S.arr1, n1)
    mm(0, j1, False, True)
    mm(1, j1, False, False)
    mm(2, j1, False, False)
    g.tensor.wait_ge(S.arr2B, n2)
    mm(1, j2, False, True)
    mm(2, j2, False, True)

    for ps, c0, c1, done, copied, _ in groups:
        g.vector.wait_ge(done, 1)
        g.vector.tensor_copy(T.ys[:, c0:c1], ps[:, 0:c1 - c0]).then_inc(copied, 1)

    for q, ks in ((g.sync, (0, 1)), (g.scalar, (2,))):
        for k in ks:
            _, c0, c1, _, copied, stored = groups[k]
            q.wait_ge(copied, 1)
            q.dma_start(T.y[:, c0:c1], T.ys[:, c0:c1]).then_inc(stored, 16)
        for k in ks:
            q.wait_ge(groups[k][5], 16)
    g.wait_ge(S.sent, sent)
